import numpy as np
import ml_dtypes


def mxq(x, axis, fmt="e4m3"):
    dtype, down = {"e4m3": (ml_dtypes.float8_e4m3fn, 7), "e5m2": (ml_dtypes.float8_e5m2, 14)}[fmt]
    v = np.moveaxis(np.asarray(x, np.float32).astype(ml_dtypes.bfloat16).astype(np.float64), axis, -1)
    blocks = v.reshape(v.shape[:-1] + (-1, 32))
    amax = np.abs(blocks).max(-1, keepdims=True)
    byte = np.maximum(np.where(amax > 0, np.frexp(amax)[1] - 1 + 127, 0) - down, 1)
    scale = np.exp2(byte - 127.0)
    codes = (blocks / scale).astype(np.float32).astype(dtype).astype(np.float64)
    return np.moveaxis((codes * scale).reshape(v.shape), -1, axis)


WIDE = False


def mx_kscale(k):
    if not WIDE:
        return np.ones(k)
    levels = np.array([10, -10, 5, -5, 0])
    if k % 512:
        return np.exp2(np.random.permutation(np.resize(levels, k // 32))).repeat(32)
    a = np.empty((k // 512, 16))
    for p in range(k // 512):
        a[p, :8] = np.random.permutation(np.resize(levels, 8))
        for g in range(8):
            far = levels[np.abs(levels - a[p, g]) >= 10]
            a[p, g + 8] = far[np.random.randint(len(far))]
    return np.exp2(a.ravel()).repeat(32)


def f64(x):
    return np.asarray(x).astype(np.float64)


def striped(idx):
    return np.tile(idx.reshape(-1, 16).T, (8, 1)).astype(np.uint16)


def unstriped(offs):
    return offs[:16].T.reshape(-1).astype(np.int64)


def striped8(idx):
    return np.concatenate([x.reshape(-1, 16).T for x in idx]).astype(np.uint16)


def runs(offs, k):
    lists = np.stack([offs[16 * r : 16 * r + 16].T.reshape(-1) for r in range(8)]).astype(np.int64)
    return lists[np.arange(k) % 512 // 64]


def pack_weight(w):
    k, n = w.shape
    w = f64(np.asarray(w, np.float32).astype(ml_dtypes.bfloat16)).reshape(k // 32, 32, n)
    amax = np.abs(w).max(1)
    byte = np.clip(np.where(amax > 0, np.frexp(amax)[1] - 1 + 127 - 7, 1), 1, 254)
    scaled = (w * np.exp2(127.0 - byte)[:, None, :]).reshape(k, n).astype(np.float32)
    words = np.ascontiguousarray(scaled.reshape(k // 512, 128, 4, n).transpose(0, 1, 3, 2)).astype(ml_dtypes.float8_e4m3fn).view(np.uint8)
    return words, np.ascontiguousarray(byte.astype(np.uint8).reshape(k // 512, 16, n))


def unpack_weight(words, scales):
    g, p, n, _ = words.shape
    vals = np.ascontiguousarray(words).view(ml_dtypes.float8_e4m3fn).astype(np.float64) * np.repeat(np.exp2(scales.astype(np.float64) - 127.0), 8, axis=1)[..., None]
    return vals.transpose(0, 1, 3, 2).reshape(g * 512, n)


K, T, S, H, W, C = 512, 2048, 256, 512, 1024, 512


def setup_inputs():
    n = np.random.standard_normal
    s = mx_kscale(K)[:, None]
    packed_xT = pack_weight(n((K, T)) * s)
    return {
        "x_words": packed_xT[0],
        "x_scales": packed_xT[1],
        "w1": (n((K, H)) / np.sqrt(K) / s).astype(np.float32),
        "gs": (np.random.uniform(0.5, 1.5, (K, 1)) / s).astype(np.float32),
        "offs": striped8(np.random.randint(0, T, (8, S))),
        "n1": striped(np.random.randint(0, S, W)),
        "cand": striped8(np.random.randint(0, T, (8, C))),
        "n2": striped(np.random.permutation(S)),
        "n3": striped(np.random.permutation(S)),
        "n4": striped(np.random.permutation(S)),
    }


def reference(x_words, x_scales, w1, gs, offs, n1, cand, n2, n3, n4):
    x_cand = unpack_weight(x_words, x_scales)[np.arange(K)[:, None], runs(cand, K)]
    xq = unpack_weight(x_words, x_scales)[np.arange(K)[:, None], runs(offs, K)]
    y = mxq(f64(w1), 0, "e4m3").T @ xq
    mb = y[:, unstriped(n1)]
    mx = mb.reshape(H, S, 4).max(axis=2)
    mn = mb.reshape(H, S, 4).min(axis=2)
    z = f64(gs) * (np.maximum(np.minimum(1.5 * y, mx), mn))
    s = 0.0625 * ((x_cand.T @ mxq(z, 0, "e4m3")))
    return np.maximum(s, s[:, unstriped(n2)]) - (np.maximum(s[:, unstriped(n3)], s[:, unstriped(n4)]))

@@ -1,0 +1,185 @@
+from contextlib import ExitStack
+
+import concourse.mybir as mybir
+
+K, T, S, H, W, C = 512, 2048, 256, 512, 1024, 512
+FLOPS = 2 * K * H * S + 2 * K * C * S
+
+F32 = mybir.dt.float32
+BF16 = mybir.dt.bfloat16
+I32 = mybir.dt.int32
+U32 = mybir.dt.uint32
+U16 = mybir.dt.uint16
+U8 = mybir.dt.uint8
+FP8X4 = mybir.dt.float8_e4m3fn_x4
+ALU = mybir.AluOpType
+COPY = mybir.ActivationFunctionType.Copy
+
+P = 128
+PACK = 4
+MEMBERS = 4
+PIECES = (128, 64, 64)
+GROUPS = (
+    (((slice(0, 1), slice(1, 2)), slice(0, 2)), ((slice(2, 3), slice(3, 4)), slice(2, 4))),
+    (((slice(0, 2), slice(2, 4)), slice(0, 4)),),
+    (((slice(0, 2),), slice(0, 2)), ((slice(2, 3), slice(3, 4)), slice(2, 4))),
+)
+Y_WINDOW = MEMBERS * max(PIECES) + 16
+S_WINDOW = S + 96
+
+
+def tile_picked_hcandgclipmix_none_p_kernel(
+    tc, x_words, x_scales, w1, gs, offs, n1, cand, n2, n3, n4, out
+):
+    nc = tc.nc
+    with ExitStack() as ctx:
+        lists = ctx.enter_context(tc.tile_pool(name="lists", bufs=1))
+        keep = ctx.enter_context(tc.tile_pool(name="keep", bufs=1))
+        psum = ctx.enter_context(tc.psum_pool(name="psum", bufs=1))
+
+        def load_list(name, src):
+            tile = lists.tile(list(src.shape), U16, name=name)
+            nc.sync.dma_start(tile[:], src)
+            return tile
+
+        gs_sb = keep.tile([P, PACK], F32, name="gs_sb")
+        nc.scalar.dma_start(gs_sb[:], gs.rearrange("(p t) o -> p (t o)", t=PACK))
+        offs_sb = load_list("offs_sb", offs)
+        scale_table = keep.tile([P, T], U8, name="scale_table")
+        scale_rows = x_scales[0].bitcast(I32)
+        nc.sync.dma_start(scale_table[:].bitcast(I32), scale_rows.unsqueeze(1).broadcast_to([16, 8, T // 4]))
+        cand_sb = load_list("cand_sb", cand)
+        n1_sb = load_list("n1_sb", n1)
+        w_raw = keep.tile([P, PACK, H], F32, name="w_raw")
+        nc.sync.dma_start(w_raw[:], w1.rearrange("(p j) c -> p j c", j=PACK))
+        word_table = keep.tile([P, T], U32, name="word_table")
+        nc.sync.dma_start(word_table[:].bitcast(I32), x_words[0].rearrange("p n t -> p (n t)").bitcast(I32))
+        n2_sb = load_list("n2_sb", n2)
+        n3_sb = load_list("n3_sb", n3)
+        n4_sb = load_list("n4_sb", n4)
+
+        y_win = [keep.tile([P, Y_WINDOW], F32, name=f"y_win{t}") for t in range(PACK)]
+        s_win = [keep.tile([P, S_WINDOW], F32, name=f"s_win{c}") for c in range(C // P)]
+        for tile in y_win + s_win:
+            nc.vector.memset(tile[:, S:], 0.0)
+
+        def gather_scales(name, offsets, n, queue):
+            picked = keep.tile([P, n], U8, name=name + "_picked")
+            nc.vector.tensor_copy(picked[:], scale_table[:].indirect(offsets[:]))
+            plane = keep.tile([P, n], U8, name=name + "_plane", align_bytes=64)
+            nc.vector.tensor_copy(plane[:].bitcast(I32), picked[:].bitcast(I32))
+            for m in range(1, 4):
+                queue.dma_start(plane[m:P:32, :].bitcast(I32), picked[8 * m : P : 32, :].bitcast(I32))
+            return plane
+
+        xq_scales = gather_scales("xq", offs_sb, S, nc.scalar)
+        xc_scales = gather_scales("xc", cand_sb, C, nc.sync)
+
+        w_codes, w_scales = [], []
+        for half in range(2):
+            grouped = keep.tile([P, 2, P, PACK], BF16, name=f"w_grouped{half}", align_bytes=64)
+            dst = grouped[:].rearrange("p t m j -> p m j t")
+            src = w_raw[:].rearrange("p j (m t) -> p m j t", t=PACK)[:, :, :, 2 * half : 2 * half + 2]
+            if half == 0:
+                nc.vector.tensor_copy(dst, src)
+            else:
+                nc.scalar.activation(dst, src, COPY)
+            codes = keep.tile([P, 2 * P], U32, name=f"w_codes{half}", align_bytes=64)
+            scales = keep.tile([P, 2 * P], U8, name=f"w_scales{half}", align_bytes=64)
+            nc.vector.quantize_mx(codes[:].bitcast(FP8X4), scales[:], grouped[:].rearrange("p t m j -> p (t m j)"))
+            w_codes.append(codes)
+            w_scales.append(scales)
+
+        xq_words = keep.tile([P, S], U32, name="xq_words", align_bytes=64)
+        nc.vector.tensor_copy(xq_words[:], word_table[:].indirect(offs_sb[:]))
+
+        for t in range(PACK):
+            bank = psum.tile([P, S], F32, name=f"y_bank{t}")
+            cols = slice((t % 2) * P, (t % 2 + 1) * P)
+            nc.tensor.matmul_mx(
+                bank[:],
+                lhsT=w_codes[t // 2][:, cols].bitcast(FP8X4),
+                lhsT_scale=w_scales[t // 2][:, cols],
+                rhs=xq_words[:].bitcast(FP8X4),
+                rhs_scale=xq_scales[:],
+                start=True,
+                stop=True,
+            )
+            if t in (0, 3):
+                nc.scalar.activation(y_win[t][:, :S], bank[:], COPY, scale=gs_sb[:, t : t + 1])
+            else:
+                nc.vector.tensor_scalar(y_win[t][:, :S], bank[:], gs_sb[:, t : t + 1], None, ALU.mult)
+
+        xc_words = keep.tile([P, C], U32, name="xc_words", align_bytes=64)
+        for h in range(2):
+            nc.vector.tensor_copy(
+                xc_words[:, h * 256 : (h + 1) * 256], word_table[:].indirect(cand_sb[:, h * 16 : (h + 1) * 16])
+            )
+
+        j0 = 0
+        s_banks = []
+        for k, w in enumerate(PIECES):
+            cols = slice(j0, j0 + w)
+            mb = keep.tile([P, PACK, w * MEMBERS], F32, name=f"mb{k}")
+            hi = keep.tile([P, PACK, w * 2], F32, name=f"hi{k}")
+            lo = keep.tile([P, PACK, w * 2], F32, name=f"lo{k}")
+            mx = keep.tile([P, PACK, w], F32, name=f"mx{k}")
+            mn = keep.tile([P, PACK, w], F32, name=f"mn{k}")
+            capped = keep.tile([P, PACK, w], F32, name=f"capped{k}")
+            members = n1_sb[:, j0 * MEMBERS // 16 : (j0 + w) * MEMBERS // 16]
+            for first_level, second_level in GROUPS[k]:
+                for ts in first_level:
+                    for t in range(ts.start, ts.stop):
+                        nc.scalar.activation(mb[:, t, :], y_win[t][:].indirect(members), COPY)
+                    nc.vector.tensor_tensor(hi[:, ts, :], mb[:, ts, 0::2], mb[:, ts, 1::2], ALU.max)
+                    nc.vector.tensor_tensor(lo[:, ts, :], mb[:, ts, 0::2], mb[:, ts, 1::2], ALU.min)
+                ts = second_level
+                nc.vector.tensor_tensor(mx[:, ts, :], hi[:, ts, 0::2], hi[:, ts, 1::2], ALU.max)
+                nc.vector.tensor_tensor(mn[:, ts, :], lo[:, ts, 0::2], lo[:, ts, 1::2], ALU.min)
+                for t in range(ts.start, ts.stop):
+                    nc.vector.scalar_tensor_tensor(
+                        capped[:, t, :], y_win[t][:, cols], 1.5, mx[:, t, :], ALU.mult, ALU.min
+                    )
+            z = keep.tile([P, w, PACK], BF16, name=f"z{k}", align_bytes=64)
+            nc.vector.tensor_tensor(
+                z[:].rearrange("p (c i) t -> p c t i", i=4),
+                capped[:].rearrange("p t (c i) -> p c t i", i=4),
+                mn[:].rearrange("p t (c i) -> p c t i", i=4),
+                ALU.max,
+            )
+            z_codes = keep.tile([P, w], U32, name=f"z_codes{k}", align_bytes=64)
+            z_scales = keep.tile([P, w], U8, name=f"z_scales{k}", align_bytes=64)
+            nc.vector.quantize_mx(z_codes[:].bitcast(FP8X4), z_scales[:], z[:].rearrange("p j t -> p (j t)"))
+            bank = psum.tile([P, C // P, w], F32, name=f"s_bank{k}")
+            for c in range(C // P):
+                rows = slice(c * P, (c + 1) * P)
+                nc.tensor.matmul_mx(
+                    bank[:, c, :],
+                    lhsT=xc_words[:, rows].bitcast(FP8X4),
+                    lhsT_scale=xc_scales[:, rows],
+                    rhs=z_codes[:].bitcast(FP8X4),
+                    rhs_scale=z_scales[:],
+                    start=True,
+                    stop=True,
+                )
+            s_banks.append((cols, bank))
+            j0 += w
+
+        for cols, bank in s_banks:
+            for c in range(C // P):
+                nc.scalar.activation(s_win[c][:, cols], bank[:, c, :], COPY, scale=0.0625)
+
+        for c in range(C // P):
+            g2 = keep.tile([P, S], F32, name=f"g2_{c}")
+            g3 = keep.tile([P, S], F32, name=f"g3_{c}")
+            g4 = keep.tile([P, S], F32, name=f"g4_{c}")
+            nc.vector.tensor_copy(g2[:], s_win[c][:].indirect(n2_sb[:]))
+            nc.scalar.activation(g3[:], s_win[c][:].indirect(n3_sb[:]), COPY)
+            nc.scalar.activation(g4[:], s_win[c][:].indirect(n4_sb[:]), COPY)
+            first = keep.tile([P, S], F32, name=f"first{c}")
+            second = keep.tile([P, S], F32, name=f"second{c}")
+            result = keep.tile([P, S], F32, name=f"result{c}")
+            nc.vector.tensor_tensor(first[:], s_win[c][:, :S], g2[:], ALU.max)
+            nc.vector.tensor_tensor(second[:], g3[:], g4[:], ALU.max)
+            nc.vector.tensor_tensor(result[:], first[:], second[:], ALU.subtract)
+            nc.sync.dma_start(out[c * P : (c + 1) * P, :], result[:])

@@ -44,17 +44,17 @@ def tile_picked_hcandgclipmix_none_p_kernel(
 
         gs_sb = keep.tile([P, PACK], F32, name="gs_sb")
         nc.scalar.dma_start(gs_sb[:], gs.rearrange("(p t) o -> p (t o)", t=PACK))
-        offs_sb = load_list("offs_sb", offs)
         scale_table = keep.tile([P, T], U8, name="scale_table")
         scale_rows = x_scales[0].bitcast(I32)
         nc.sync.dma_start(scale_table[:].bitcast(I32), scale_rows.unsqueeze(1).broadcast_to([16, 8, T // 4]))
+        offs_sb = load_list("offs_sb", offs)
         cand_sb = load_list("cand_sb", cand)
         n1_sb = load_list("n1_sb", n1)
+        n2_sb = load_list("n2_sb", n2)
         w_raw = keep.tile([P, PACK, H], F32, name="w_raw")
         nc.sync.dma_start(w_raw[:], w1.rearrange("(p j) c -> p j c", j=PACK))
         word_table = keep.tile([P, T], U32, name="word_table")
         nc.sync.dma_start(word_table[:].bitcast(I32), x_words[0].rearrange("p n t -> p (n t)").bitcast(I32))
-        n2_sb = load_list("n2_sb", n2)
         n3_sb = load_list("n3_sb", n3)
         n4_sb = load_list("n4_sb", n4)
 
@@ -64,11 +64,11 @@ def tile_picked_hcandgclipmix_none_p_kernel(
             nc.vector.memset(tile[:, S:], 0.0)
 
         def gather_scales(name, offsets, n, queue):
+            plane = keep.tile([P, n], U8, name=name + "_plane", align_bytes=64)
+            nc.vector.memset(plane[:].bitcast(I32), 0)
             picked = keep.tile([P, n], U8, name=name + "_picked")
             nc.vector.tensor_copy(picked[:], scale_table[:].indirect(offsets[:]))
-            plane = keep.tile([P, n], U8, name=name + "_plane", align_bytes=64)
-            nc.vector.tensor_copy(plane[:].bitcast(I32), picked[:].bitcast(I32))
-            for m in range(1, 4):
+            for m in range(4):
                 queue.dma_start(plane[m:P:32, :].bitcast(I32), picked[8 * m : P : 32, :].bitcast(I32))
             return plane
 
@@ -105,7 +105,7 @@ def tile_picked_hcandgclipmix_none_p_kernel(
                 start=True,
                 stop=True,
             )
-            if t in (0, 3):
+            if t == 0:
                 nc.scalar.activation(y_win[t][:, :S], bank[:], COPY, scale=gs_sb[:, t : t + 1])
             else:
                 nc.vector.tensor_scalar(y_win[t][:, :S], bank[:], gs_sb[:, t : t + 1], None, ALU.mult)
@@ -120,22 +120,28 @@ def tile_picked_hcandgclipmix_none_p_kernel(
         s_banks = []
         for k, w in enumerate(PIECES):
             cols = slice(j0, j0 + w)
-            mb = keep.tile([P, PACK, w * MEMBERS], F32, name=f"mb{k}")
-            hi = keep.tile([P, PACK, w * 2], F32, name=f"hi{k}")
-            lo = keep.tile([P, PACK, w * 2], F32, name=f"lo{k}")
+            mb = keep.tile([P, PACK, w, MEMBERS], F32, name=f"mb{k}")
+            hi = keep.tile([P, PACK, w, 2], F32, name=f"hi{k}")
+            lo = keep.tile([P, PACK, w, 2], F32, name=f"lo{k}")
             mx = keep.tile([P, PACK, w], F32, name=f"mx{k}")
             mn = keep.tile([P, PACK, w], F32, name=f"mn{k}")
             capped = keep.tile([P, PACK, w], F32, name=f"capped{k}")
-            members = n1_sb[:, j0 * MEMBERS // 16 : (j0 + w) * MEMBERS // 16]
             for first_level, second_level in GROUPS[k]:
                 for ts in first_level:
-                    for t in range(ts.start, ts.stop):
-                        nc.scalar.activation(mb[:, t, :], y_win[t][:].indirect(members), COPY)
-                    nc.vector.tensor_tensor(hi[:, ts, :], mb[:, ts, 0::2], mb[:, ts, 1::2], ALU.max)
-                    nc.vector.tensor_tensor(lo[:, ts, :], mb[:, ts, 0::2], mb[:, ts, 1::2], ALU.min)
+                    parts = 2 if (k, ts.start) == (0, 0) else 1
+                    n = w // parts
+                    for h in range(parts):
+                        js = slice(h * n, (h + 1) * n)
+                        members = n1_sb[:, (j0 + h * n) * MEMBERS // 16 : (j0 + (h + 1) * n) * MEMBERS // 16]
+                        for t in range(ts.start, ts.stop):
+                            nc.scalar.activation(
+                                mb[:, t, js].rearrange("p j m -> p (j m)"), y_win[t][:].indirect(members), COPY
+                            )
+                        nc.vector.tensor_tensor(hi[:, ts, js], mb[:, ts, js, 0:2], mb[:, ts, js, 2:4], ALU.max)
+                        nc.vector.tensor_tensor(lo[:, ts, js], mb[:, ts, js, 0:2], mb[:, ts, js, 2:4], ALU.min)
                 ts = second_level
-                nc.vector.tensor_tensor(mx[:, ts, :], hi[:, ts, 0::2], hi[:, ts, 1::2], ALU.max)
-                nc.vector.tensor_tensor(mn[:, ts, :], lo[:, ts, 0::2], lo[:, ts, 1::2], ALU.min)
+                nc.vector.tensor_tensor(mx[:, ts, :], hi[:, ts, :, 0], hi[:, ts, :, 1], ALU.max)
+                nc.vector.tensor_tensor(mn[:, ts, :], lo[:, ts, :, 0], lo[:, ts, :, 1], ALU.min)
                 for t in range(ts.start, ts.stop):
                     nc.vector.scalar_tensor_tensor(
                         capped[:, t, :], y_win[t][:, cols], 1.5, mx[:, t, :], ALU.mult, ALU.min
@@ -169,17 +175,25 @@ def tile_picked_hcandgclipmix_none_p_kernel(
             for c in range(C // P):
                 nc.scalar.activation(s_win[c][:, cols], bank[:, c, :], COPY, scale=0.0625)
 
-        for c in range(C // P):
+        tiles = C // P
+        for c in range(tiles):
+            last = c == tiles - 1
             g2 = keep.tile([P, S], F32, name=f"g2_{c}")
             g3 = keep.tile([P, S], F32, name=f"g3_{c}")
             g4 = keep.tile([P, S], F32, name=f"g4_{c}")
-            nc.vector.tensor_copy(g2[:], s_win[c][:].indirect(n2_sb[:]))
-            nc.scalar.activation(g3[:], s_win[c][:].indirect(n3_sb[:]), COPY)
-            nc.scalar.activation(g4[:], s_win[c][:].indirect(n4_sb[:]), COPY)
             first = keep.tile([P, S], F32, name=f"first{c}")
             second = keep.tile([P, S], F32, name=f"second{c}")
             result = keep.tile([P, S], F32, name=f"result{c}")
+            nc.vector.tensor_copy(g2[:], s_win[c][:].indirect(n2_sb[:]))
             nc.vector.tensor_tensor(first[:], s_win[c][:, :S], g2[:], ALU.max)
-            nc.vector.tensor_tensor(second[:], g3[:], g4[:], ALU.max)
-            nc.vector.tensor_tensor(result[:], first[:], second[:], ALU.subtract)
-            nc.sync.dma_start(out[c * P : (c + 1) * P, :], result[:])
+            parts = 2 if last else 1
+            n = S // parts
+            for h in range(parts):
+                cols = slice(h * n, (h + 1) * n)
+                entries = slice(h * n // 16, (h + 1) * n // 16)
+                nc.scalar.activation(g3[:, cols], s_win[c][:].indirect(n3_sb[:, entries]), COPY)
+                nc.scalar.activation(g4[:, cols], s_win[c][:].indirect(n4_sb[:, entries]), COPY)
+                nc.vector.tensor_tensor(second[:, cols], g3[:, cols], g4[:, cols], ALU.max)
+                engine = nc.vector if last else nc.gpsimd
+                engine.tensor_tensor(result[:, cols], first[:, cols], second[:, cols], ALU.subtract)
+                nc.sync.dma_start(out[c * P : (c + 1) * P, cols], result[:, cols])

from contextlib import ExitStack

import concourse.mybir as mybir

K, T, S, H, W, C = 512, 2048, 256, 512, 1024, 512
FLOPS = 2 * K * H * S + 2 * K * C * S

F32 = mybir.dt.float32
BF16 = mybir.dt.bfloat16
I32 = mybir.dt.int32
U32 = mybir.dt.uint32
U16 = mybir.dt.uint16
U8 = mybir.dt.uint8
FP8X4 = mybir.dt.float8_e4m3fn_x4
ALU = mybir.AluOpType
COPY = mybir.ActivationFunctionType.Copy

P = 128
PACK = 4
MEMBERS = 4
PIECES = (128, 64, 64)
GROUPS = (
    (((slice(0, 1), slice(1, 2)), slice(0, 2)), ((slice(2, 3), slice(3, 4)), slice(2, 4))),
    (((slice(0, 2), slice(2, 4)), slice(0, 4)),),
    (((slice(0, 2),), slice(0, 2)), ((slice(2, 3), slice(3, 4)), slice(2, 4))),
)
Y_WINDOW = MEMBERS * max(PIECES) + 16
S_WINDOW = S + 96


def tile_picked_hcandgclipmix_none_p_kernel(
    tc, x_words, x_scales, w1, gs, offs, n1, cand, n2, n3, n4, out
):
    nc = tc.nc
    with ExitStack() as ctx:
        lists = ctx.enter_context(tc.tile_pool(name="lists", bufs=1))
        keep = ctx.enter_context(tc.tile_pool(name="keep", bufs=1))
        psum = ctx.enter_context(tc.psum_pool(name="psum", bufs=1))

        def load_list(name, src):
            tile = lists.tile(list(src.shape), U16, name=name)
            nc.sync.dma_start(tile[:], src)
            return tile

        gs_sb = keep.tile([P, PACK], F32, name="gs_sb")
        nc.scalar.dma_start(gs_sb[:], gs.rearrange("(p t) o -> p (t o)", t=PACK))
        scale_table = keep.tile([P, T], U8, name="scale_table")
        scale_rows = x_scales[0].bitcast(I32)
        nc.sync.dma_start(scale_table[:].bitcast(I32), scale_rows.unsqueeze(1).broadcast_to([16, 8, T // 4]))
        offs_sb = load_list("offs_sb", offs)
        cand_sb = load_list("cand_sb", cand)
        n1_sb = load_list("n1_sb", n1)
        n2_sb = load_list("n2_sb", n2)
        w_raw = keep.tile([P, PACK, H], F32, name="w_raw")
        nc.sync.dma_start(w_raw[:], w1.rearrange("(p j) c -> p j c", j=PACK))
        word_table = keep.tile([P, T], U32, name="word_table")
        nc.sync.dma_start(word_table[:].bitcast(I32), x_words[0].rearrange("p n t -> p (n t)").bitcast(I32))
        n3_sb = load_list("n3_sb", n3)
        n4_sb = load_list("n4_sb", n4)

        y_win = [keep.tile([P, Y_WINDOW], F32, name=f"y_win{t}") for t in range(PACK)]
        s_win = [keep.tile([P, S_WINDOW], F32, name=f"s_win{c}") for c in range(C // P)]
        for tile in y_win + s_win:
            nc.vector.memset(tile[:, S:], 0.0)

        def gather_scales(name, offsets, n, queue):
            plane = keep.tile([P, n], U8, name=name + "_plane", align_bytes=64)
            nc.vector.memset(plane[:].bitcast(I32), 0)
            picked = keep.tile([P, n], U8, name=name + "_picked")
            nc.vector.tensor_copy(picked[:], scale_table[:].indirect(offsets[:]))
            for m in range(4):
                queue.dma_start(plane[m:P:32, :].bitcast(I32), picked[8 * m : P : 32, :].bitcast(I32))
            return plane

        xq_scales = gather_scales("xq", offs_sb, S, nc.scalar)
        xc_scales = gather_scales("xc", cand_sb, C, nc.sync)

        w_codes, w_scales = [], []
        for half in range(2):
            grouped = keep.tile([P, 2, P, PACK], BF16, name=f"w_grouped{half}", align_bytes=64)
            dst = grouped[:].rearrange("p t m j -> p m j t")
            src = w_raw[:].rearrange("p j (m t) -> p m j t", t=PACK)[:, :, :, 2 * half : 2 * half + 2]
            if half == 0:
                nc.vector.tensor_copy(dst, src)
            else:
                nc.scalar.activation(dst, src, COPY)
            codes = keep.tile([P, 2 * P], U32, name=f"w_codes{half}", align_bytes=64)
            scales = keep.tile([P, 2 * P], U8, name=f"w_scales{half}", align_bytes=64)
            nc.vector.quantize_mx(codes[:].bitcast(FP8X4), scales[:], grouped[:].rearrange("p t m j -> p (t m j)"))
            w_codes.append(codes)
            w_scales.append(scales)

        xq_words = keep.tile([P, S], U32, name="xq_words", align_bytes=64)
        nc.vector.tensor_copy(xq_words[:], word_table[:].indirect(offs_sb[:]))

        for t in range(PACK):
            bank = psum.tile([P, S], F32, name=f"y_bank{t}")
            cols = slice((t % 2) * P, (t % 2 + 1) * P)
            nc.tensor.matmul_mx(
                bank[:],
                lhsT=w_codes[t // 2][:, cols].bitcast(FP8X4),
                lhsT_scale=w_scales[t // 2][:, cols],
                rhs=xq_words[:].bitcast(FP8X4),
                rhs_scale=xq_scales[:],
                start=True,
                stop=True,
            )
            if t == 0:
                nc.scalar.activation(y_win[t][:, :S], bank[:], COPY, scale=gs_sb[:, t : t + 1])
            else:
                nc.vector.tensor_scalar(y_win[t][:, :S], bank[:], gs_sb[:, t : t + 1], None, ALU.mult)

        xc_words = keep.tile([P, C], U32, name="xc_words", align_bytes=64)
        for h in range(2):
            nc.vector.tensor_copy(
                xc_words[:, h * 256 : (h + 1) * 256], word_table[:].indirect(cand_sb[:, h * 16 : (h + 1) * 16])
            )

        j0 = 0
        s_banks = []
        for k, w in enumerate(PIECES):
            cols = slice(j0, j0 + w)
            mb = keep.tile([P, PACK, w, MEMBERS], F32, name=f"mb{k}")
            hi = keep.tile([P, PACK, w, 2], F32, name=f"hi{k}")
            lo = keep.tile([P, PACK, w, 2], F32, name=f"lo{k}")
            mx = keep.tile([P, PACK, w], F32, name=f"mx{k}")
            mn = keep.tile([P, PACK, w], F32, name=f"mn{k}")
            capped = keep.tile([P, PACK, w], F32, name=f"capped{k}")
            for first_level, second_level in GROUPS[k]:
                for ts in first_level:
                    parts = 2 if (k, ts.start) == (0, 0) else 1
                    n = w // parts
                    for h in range(parts):
                        js = slice(h * n, (h + 1) * n)
                        members = n1_sb[:, (j0 + h * n) * MEMBERS // 16 : (j0 + (h + 1) * n) * MEMBERS // 16]
                        for t in range(ts.start, ts.stop):
                            nc.scalar.activation(
                                mb[:, t, js].rearrange("p j m -> p (j m)"), y_win[t][:].indirect(members), COPY
                            )
                        nc.vector.tensor_tensor(hi[:, ts, js], mb[:, ts, js, 0:2], mb[:, ts, js, 2:4], ALU.max)
                        nc.vector.tensor_tensor(lo[:, ts, js], mb[:, ts, js, 0:2], mb[:, ts, js, 2:4], ALU.min)
                ts = second_level
                nc.vector.tensor_tensor(mx[:, ts, :], hi[:, ts, :, 0], hi[:, ts, :, 1], ALU.max)
                nc.vector.tensor_tensor(mn[:, ts, :], lo[:, ts, :, 0], lo[:, ts, :, 1], ALU.min)
                for t in range(ts.start, ts.stop):
                    nc.vector.scalar_tensor_tensor(
                        capped[:, t, :], y_win[t][:, cols], 1.5, mx[:, t, :], ALU.mult, ALU.min
                    )
            z = keep.tile([P, w, PACK], BF16, name=f"z{k}", align_bytes=64)
            nc.vector.tensor_tensor(
                z[:].rearrange("p (c i) t -> p c t i", i=4),
                capped[:].rearrange("p t (c i) -> p c t i", i=4),
                mn[:].rearrange("p t (c i) -> p c t i", i=4),
                ALU.max,
            )
            z_codes = keep.tile([P, w], U32, name=f"z_codes{k}", align_bytes=64)
            z_scales = keep.tile([P, w], U8, name=f"z_scales{k}", align_bytes=64)
            nc.vector.quantize_mx(z_codes[:].bitcast(FP8X4), z_scales[:], z[:].rearrange("p j t -> p (j t)"))
            bank = psum.tile([P, C // P, w], F32, name=f"s_bank{k}")
            for c in range(C // P):
                rows = slice(c * P, (c + 1) * P)
                nc.tensor.matmul_mx(
                    bank[:, c, :],
                    lhsT=xc_words[:, rows].bitcast(FP8X4),
                    lhsT_scale=xc_scales[:, rows],
                    rhs=z_codes[:].bitcast(FP8X4),
                    rhs_scale=z_scales[:],
                    start=True,
                    stop=True,
                )
            s_banks.append((cols, bank))
            j0 += w

        for cols, bank in s_banks:
            for c in range(C // P):
                nc.scalar.activation(s_win[c][:, cols], bank[:, c, :], COPY, scale=0.0625)

        tiles = C // P
        for c in range(tiles):
            last = c == tiles - 1
            g2 = keep.tile([P, S], F32, name=f"g2_{c}")
            g3 = keep.tile([P, S], F32, name=f"g3_{c}")
            g4 = keep.tile([P, S], F32, name=f"g4_{c}")
            first = keep.tile([P, S], F32, name=f"first{c}")
            second = keep.tile([P, S], F32, name=f"second{c}")
            result = keep.tile([P, S], F32, name=f"result{c}")
            nc.vector.tensor_copy(g2[:], s_win[c][:].indirect(n2_sb[:]))
            nc.vector.tensor_tensor(first[:], s_win[c][:, :S], g2[:], ALU.max)
            parts = 2 if last else 1
            n = S // parts
            for h in range(parts):
                cols = slice(h * n, (h + 1) * n)
                entries = slice(h * n // 16, (h + 1) * n // 16)
                nc.scalar.activation(g3[:, cols], s_win[c][:].indirect(n3_sb[:, entries]), COPY)
                nc.scalar.activation(g4[:, cols], s_win[c][:].indirect(n4_sb[:, entries]), COPY)
                nc.vector.tensor_tensor(second[:, cols], g3[:, cols], g4[:, cols], ALU.max)
                engine = nc.vector if last else nc.gpsimd
                engine.tensor_tensor(result[:, cols], first[:, cols], second[:, cols], ALU.subtract)
                nc.sync.dma_start(out[c * P : (c + 1) * P, cols], result[:, cols])
